import numpy as np
import ml_dtypes


def mxq(x, axis, fmt="e4m3"):
    dtype, down = {"e4m3": (ml_dtypes.float8_e4m3fn, 7), "e5m2": (ml_dtypes.float8_e5m2, 14)}[fmt]
    v = np.moveaxis(np.asarray(x, np.float32).astype(ml_dtypes.bfloat16).astype(np.float64), axis, -1)
    blocks = v.reshape(v.shape[:-1] + (-1, 32))
    amax = np.abs(blocks).max(-1, keepdims=True)
    byte = np.maximum(np.where(amax > 0, np.frexp(amax)[1] - 1 + 127, 0) - down, 1)
    scale = np.exp2(byte - 127.0)
    codes = (blocks / scale).astype(np.float32).astype(dtype).astype(np.float64)
    return np.moveaxis((codes * scale).reshape(v.shape), -1, axis)


WIDE = False


def mx_kscale(k, group=512):
    if not WIDE:
        return np.ones(k)
    levels = np.array([10, -10, 5, -5, 0])
    if group != 512:
        return np.exp2(np.random.permutation(np.resize(levels, k // group))).repeat(group)
    if k % 512:
        return np.exp2(np.random.permutation(np.resize(levels, k // 32))).repeat(32)
    a = np.empty((k // 512, 16))
    for p in range(k // 512):
        a[p, :8] = np.random.permutation(np.resize(levels, 8))
        for g in range(8):
            far = levels[np.abs(levels - a[p, g]) >= 10]
            a[p, g + 8] = far[np.random.randint(len(far))]
    return np.exp2(a.ravel()).repeat(32)


def f64(x):
    return np.asarray(x).astype(np.float64)


def sigmoid(v):
    return 1.0 / (1.0 + np.exp(-v))


def bf(x):
    return np.asarray(x, np.float32).astype(ml_dtypes.bfloat16)


def planes(Y):
    r, m = Y.shape
    b = f64(bf(Y)).reshape(r // 32, 32, m)
    amax = np.abs(b).max(1)
    byte = np.clip(np.where(amax > 0, np.frexp(amax)[1] - 1 + 127 - 7, 1), 1, 254)
    codes = (b * np.exp2(127.0 - byte)[:, None, :]).reshape(r, m).astype(np.float32).astype(ml_dtypes.float8_e4m3fn).view(np.uint8)
    words = codes.reshape(r // 512, 128, 4, m).transpose(0, 1, 3, 2)
    return np.ascontiguousarray(words), np.ascontiguousarray(byte.astype(np.uint8).reshape(r // 512, 16, m))


G, D, M, N = 2, 256, 256, 512


def setup_inputs():
    n = np.random.standard_normal
    s_d = mx_kscale(D, 0)
    return {
        "h": (n((G, D, N)) * s_d[:, None]).astype(np.float32),
        "wf": (n((G, D, M)) / np.sqrt(D) / s_d[:, None]).astype(np.float32),
        "wa": (n((G, D, M)) / np.sqrt(D) / s_d[:, None]).astype(np.float32),
        "wb": (n((G, D, M)) / np.sqrt(D) / s_d[:, None]).astype(np.float32),
        "ts": (n((G, M, N))).astype(np.float32),
        "bf": (0.5 * n((G, M, 1))).astype(np.float32),
    }


def reference(h, wf, wa, wb, ts, bf):
    wfq = mxq(f64(wf), 1, "e4m3")
    hq = mxq(f64(h), 1, "e4m3")
    zf = wfq.transpose(0, 2, 1) @ hq
    waq = mxq(f64(wa), 1, "e4m3")
    za = waq.transpose(0, 2, 1) @ hq
    wbq = mxq(f64(wb), 1, "e4m3")
    zb = wbq.transpose(0, 2, 1) @ hq
    s = sigmoid((-(zf + f64(bf))) * f64(ts))
    y = s * np.tanh(za) + (1.0 - s) * np.tanh(zb)
    Y = y.reshape(G * M, N)
    words, scales = planes(Y)
    return Y, words, scales

from contextlib import ExitStack

import concourse.mybir as mybir

G, D, M, N = 2, 256, 256, 512
FLOPS = 3 * 2 * G * D * M * N

F32 = mybir.dt.float32
BF16 = mybir.dt.bfloat16
I32 = mybir.dt.int32
U32 = mybir.dt.uint32
U8 = mybir.dt.uint8
FP8X4 = mybir.dt.float8_e4m3fn_x4
ACT = mybir.ActivationFunctionType
ALU = mybir.AluOpType

P = 128
R = 64
PACK = 4
W = 128
HALF = 256
W_SPLIT = 42


def tile_rows_pl_cell_cfc_kernel(tc, h, wf, wa, wb, ts, bf, out_0, out_1, out_2):
    nc = tc.nc
    with ExitStack() as ctx:
        sb = ctx.enter_context(tc.tile_pool(name="sb", bufs=1))
        ps = ctx.enter_context(tc.psum_pool(name="ps", bufs=1))
        ctx.enter_context(tc.manual_schedule())

        weights = {"a": wa, "b": wb, "f": wf}
        h_raw = sb.tile([P, PACK, N], F32, name="h_raw")
        w_raw = {k: sb.tile([P, PACK, M], F32, name="w_raw_" + k) for k in "abf"}
        ts_sb = [sb.tile([P, PACK, HALF], F32, name="ts_%d" % g) for g in range(G)]
        bias = sb.tile([P, G, 8], F32, name="bias")
        h_bf = [sb.tile([P, 2 * W * PACK], BF16, name="h_bf_%d" % c, align_bytes=64) for c in range(2)]
        h_codes = [sb.tile([P, 2 * W], U32, name="h_codes_%d" % c, align_bytes=64) for c in range(2)]
        h_scales = [sb.tile([P, 2 * W], U8, name="h_scales_%d" % c, align_bytes=64) for c in range(2)]
        w_bf = {k: sb.tile([P, M * PACK], BF16, name="w_bf_" + k, align_bytes=64) for k in "abf"}
        w_codes = {k: sb.tile([P, 9 * R], U32, name="w_codes_" + k, align_bytes=64) for k in "abf"}
        w_scales = {k: sb.tile([P, 9 * R], U8, name="w_scales_" + k, align_bytes=64) for k in "abf"}
        banks = [[ps.tile([P, PACK, W], F32, name="bank_%d_%d" % (g, i)) for i in range(4)] for g in range(G)]
        chunks = [(g, c) for c in range(2) for g in range(G)]
        work = {}
        for name in ("ta", "tb", "arg", "gate", "d", "e", "y"):
            for g, c in chunks:
                work[name, g, c] = sb.tile([P, PACK, W], F32, name="%s_%d_%d" % (name, g, c))
        y_bf = {}
        for g, c in chunks:
            y_bf[g, c] = sb.tile([P, W * PACK], BF16, name="y_bf_%d_%d" % (g, c), align_bytes=64)
        y_codes = sb.tile([P, N], U32, name="y_codes", align_bytes=64)
        y_scales = sb.tile([P, N], U8, name="y_scales", align_bytes=64)
        warm = sb.tile([P, 8], F32, name="warm")
        warm_out = sb.tile([P, 8], F32, name="warm_out")

        bank_of = {("a", 0): 0, ("b", 0): 1, ("f", 0): 2, ("a", 1): 3, ("b", 1): 0, ("f", 1): 1}

        def load_ts(queue, g, b):
            queue.dma_start(
                out=ts_sb[g][R * b : R * b + R],
                in_=ts[g, :, HALF * b : HALF * b + HALF].rearrange("(p u) n -> p u n", u=PACK),
            )

        def interleave(engine_copy, dst, src):
            engine_copy(
                out=dst.rearrange("p (n i x) -> p n x i", i=4, x=PACK),
                in_=src.rearrange("p x (n i) -> p n x i", i=4),
            )

        def round_h(engine_copy, c, b):
            n0 = HALF * b + W * c
            interleave(engine_copy, h_bf[c][:, W * PACK * b : W * PACK * (b + 1)], h_raw[:, :, n0 : n0 + W])

        def quantize_h(c):
            nc.vector.quantize_mx(out=h_codes[c][:].bitcast(FP8X4), scales=h_scales[c][:], in_=h_bf[c][:])

        def round_w(engine_copy, k, q0, q1):
            engine_copy(
                out=w_bf[k][:].rearrange("p (u q x) -> p q u x", u=PACK, x=PACK)[:, q0:q1],
                in_=w_raw[k][:].rearrange("p x (q u) -> p q u x", u=PACK)[:, q0:q1],
            )

        def quantize_w(k):
            for u in range(PACK):
                cols = slice(R * (2 * u + 1), R * (2 * u + 2))
                nc.vector.quantize_mx(
                    out=w_codes[k][:, cols].bitcast(FP8X4),
                    scales=w_scales[k][:, cols],
                    in_=w_bf[k][:, R * PACK * u : R * PACK * (u + 1)],
                )

        def product(k, c):
            for u in range(PACK):
                for b in range(2):
                    w0 = R * (2 * u + 1 - b)
                    for g in range(G):
                        rows = slice(R * g, R * g + R)
                        nc.tensor.matmul_mx(
                            out=banks[g][bank_of[k, c]][:, u, :],
                            lhsT=w_codes[k][rows, w0 : w0 + P].bitcast(FP8X4),
                            lhsT_scale=w_scales[k][rows, w0 : w0 + P],
                            rhs=h_codes[c][rows, W * b : W * b + W].bitcast(FP8X4),
                            rhs_scale=h_scales[c][rows, W * b : W * b + W],
                            start=(b == 0),
                            stop=(b == 1),
                        )

        def tanh_of(k, g, c):
            nc.scalar.activation(out=work["t" + k, g, c][:], in_=banks[g][bank_of[k, c]][:], func=ACT.Tanh)

        def gate_arg(g, c):
            for u in range(PACK):
                nc.vector.scalar_tensor_tensor(
                    out=work["arg", g, c][:, u, :],
                    in0=banks[g][bank_of["f", c]][:, u, :],
                    scalar=bias[:, g, u : u + 1],
                    in1=ts_sb[g][:, u, W * c : W * c + W],
                    op0=ALU.add,
                    op1=ALU.mult,
                )

        def gate(g, c):
            nc.scalar.activation(out=work["gate", g, c][:], in_=work["arg", g, c][:], func=ACT.Tanh, scale=0.5)

        def diff(g, c):
            nc.vector.tensor_tensor(
                out=work["d", g, c][:], in0=work["ta", g, c][:], in1=work["tb", g, c][:], op=ALU.subtract
            )

        def weigh(g, c):
            nc.vector.scalar_tensor_tensor(
                out=work["e", g, c][:],
                in0=work["gate", g, c][:],
                scalar=1.0,
                in1=work["d", g, c][:],
                op0=ALU.subtract,
                op1=ALU.mult,
            )

        def mix(g, c):
            nc.vector.scalar_tensor_tensor(
                out=work["y", g, c][:],
                in0=work["e", g, c][:],
                scalar=-0.5,
                in1=work["tb", g, c][:],
                op0=ALU.mult,
                op1=ALU.add,
            )

        def store_y(queue, g, c, b):
            n0 = HALF * b + W * c
            queue.dma_start(
                out=out_0[M * g : M * g + M, n0 : n0 + W].rearrange("(p u) n -> p u n", u=PACK),
                in_=work["y", g, c][R * b : R * b + R],
            )

        def round_y(engine_copy, g, c):
            interleave(engine_copy, y_bf[g, c][:], work["y", g, c][:])

        def quantize_y(g, c):
            cols = slice(HALF * g + W * c, HALF * g + W * c + W)
            nc.vector.quantize_mx(out=y_codes[:, cols].bitcast(FP8X4), scales=y_scales[:, cols], in_=y_bf[g, c][:])

        words = out_1.rearrange("r (g p) n t -> p (r g) (n t)", g=G).bitcast(I32)
        scale_rows = out_2.rearrange("r (g v t) n -> v t (r g) n", g=G, v=2).bitcast(I32)

        def store_words(queue, b):
            queue.dma_start(
                out=words[:, :, HALF * b : HALF * b + HALF],
                in_=y_codes[R * b : R * b + R, :].bitcast(I32).rearrange("p (g n) -> p g n", g=G),
            )

        def store_scales(queue, b, v):
            p0 = R * b + 32 * v
            queue.dma_start(
                out=scale_rows[v, :, :, R * b : R * b + R],
                in_=y_scales[p0 : p0 + 4, :].bitcast(I32).rearrange("p (g n) -> p g n", g=G),
            )

        vcopy = nc.vector.tensor_copy
        scopy = nc.scalar.copy

        nc.sync.dma_start(out=h_raw[:], in_=h.rearrange("g (p x) n -> (g p) x n", x=PACK))
        for k in "abf":
            nc.sync.dma_start(out=w_raw[k][:], in_=weights[k].rearrange("g (p x) m -> (g p) x m", x=PACK))
        load_ts(nc.sync, 0, 0)
        load_ts(nc.sync, 1, 0)
        for b in range(2):
            nc.gpsimd.dma_start(
                out=bias[R * b : R * b + R, :, 0:PACK], in_=bf.rearrange("g (p u) o -> p g (u o)", u=PACK)
            )
        nc.vector.memset(warm[:], 0.0)
        nc.scalar.activation(out=warm_out[:], in_=warm[:], func=ACT.Tanh)
        for k in "abf":
            nc.vector.memset(w_codes[k][:], 0)
            nc.vector.memset(w_scales[k][:].bitcast(U32), 0)

        round_h(vcopy, 0, 0)
        round_h(scopy, 0, 1)
        round_h(vcopy, 1, 0)
        quantize_h(0)
        round_h(scopy, 1, 1)
        round_w(vcopy, "a", 0, W_SPLIT)
        round_w(scopy, "a", W_SPLIT, R)
        load_ts(nc.scalar, 0, 1)
        quantize_h(1)
        quantize_w("a")
        product("a", 0)
        round_w(vcopy, "b", 0, W_SPLIT)
        round_w(scopy, "b", W_SPLIT, R)
        load_ts(nc.scalar, 1, 1)
        quantize_w("b")
        product("b", 0)
        round_w(vcopy, "f", 0, R)
        quantize_w("f")
        product("f", 0)
        product("a", 1)
        tanh_of("a", 0, 0)
        tanh_of("a", 1, 0)
        tanh_of("b", 0, 0)
        tanh_of("b", 1, 0)
        product("b", 1)
        product("f", 1)
        diff(0, 0)
        diff(1, 0)
        gate_arg(0, 0)
        gate_arg(1, 0)
        gate(0, 0)
        gate(1, 0)
        tanh_of("a", 0, 1)
        tanh_of("a", 1, 1)
        tanh_of("b", 0, 1)
        tanh_of("b", 1, 1)
        weigh(0, 0)
        weigh(1, 0)
        mix(0, 0)
        mix(1, 0)
        for g in range(G):
            for b in range(2):
                store_y(nc.sync, g, 0, b)
        gate_arg(0, 1)
        gate_arg(1, 1)
        gate(0, 1)
        gate(1, 1)
        round_y(scopy, 0, 0)
        round_y(scopy, 1, 0)
        diff(0, 1)
        diff(1, 1)
        weigh(0, 1)
        weigh(1, 1)
        mix(0, 1)
        mix(1, 1)
        store_y(nc.sync, 0, 1, 0)
        store_y(nc.sync, 0, 1, 1)
        round_y(scopy, 0, 1)
        store_y(nc.sync, 1, 1, 0)
        store_y(nc.scalar, 1, 1, 1)
        quantize_y(0, 0)
        quantize_y(1, 0)
        round_y(vcopy, 1, 1)
        quantize_y(0, 1)
        quantize_y(1, 1)
        store_words(nc.sync, 0)
        store_words(nc.scalar, 1)
        for v in range(2):
            store_scales(nc.sync, 0, v)
            store_scales(nc.scalar, 1, v)
